import numpy as np
import ml_dtypes


def mxq(x, axis, fmt="e4m3"):
    dtype, down = {"e4m3": (ml_dtypes.float8_e4m3fn, 7), "e5m2": (ml_dtypes.float8_e5m2, 14)}[fmt]
    v = np.moveaxis(np.asarray(x, np.float32).astype(ml_dtypes.bfloat16).astype(np.float64), axis, -1)
    blocks = v.reshape(v.shape[:-1] + (-1, 32))
    amax = np.abs(blocks).max(-1, keepdims=True)
    byte = np.maximum(np.where(amax > 0, np.frexp(amax)[1] - 1 + 127, 0) - down, 1)
    scale = np.exp2(byte - 127.0)
    codes = (blocks / scale).astype(np.float32).astype(dtype).astype(np.float64)
    return np.moveaxis((codes * scale).reshape(v.shape), -1, axis)


WIDE = False


def mx_kscale(k):
    if not WIDE:
        return np.ones(k)
    levels = np.array([10, -10, 5, -5, 0])
    if k % 512:
        return np.exp2(np.random.permutation(np.resize(levels, k // 32))).repeat(32)
    a = np.empty((k // 512, 16))
    for p in range(k // 512):
        a[p, :8] = np.random.permutation(np.resize(levels, 8))
        for g in range(8):
            far = levels[np.abs(levels - a[p, g]) >= 10]
            a[p, g + 8] = far[np.random.randint(len(far))]
    return np.exp2(a.ravel()).repeat(32)


def f64(x):
    return np.asarray(x).astype(np.float64)


def striped(idx):
    return np.tile(idx.reshape(-1, 16).T, (8, 1)).astype(np.uint16)


def unstriped(offs):
    return offs[:16].T.reshape(-1).astype(np.int64)


def striped8(idx):
    return np.concatenate([x.reshape(-1, 16).T for x in idx]).astype(np.uint16)


def runs(offs, k):
    lists = np.stack([offs[16 * r : 16 * r + 16].T.reshape(-1) for r in range(8)]).astype(np.int64)
    return lists[np.arange(k) % 512 // 64]


def pack_weight(w):
    k, n = w.shape
    w = f64(np.asarray(w, np.float32).astype(ml_dtypes.bfloat16)).reshape(k // 32, 32, n)
    amax = np.abs(w).max(1)
    byte = np.clip(np.where(amax > 0, np.frexp(amax)[1] - 1 + 127 - 7, 1), 1, 254)
    scaled = (w * np.exp2(127.0 - byte)[:, None, :]).reshape(k, n).astype(np.float32)
    words = np.ascontiguousarray(scaled.reshape(k // 512, 128, 4, n).transpose(0, 1, 3, 2)).astype(ml_dtypes.float8_e4m3fn).view(np.uint8)
    return words, np.ascontiguousarray(byte.astype(np.uint8).reshape(k // 512, 16, n))


def unpack_weight(words, scales):
    g, p, n, _ = words.shape
    vals = np.ascontiguousarray(words).view(ml_dtypes.float8_e4m3fn).astype(np.float64) * np.repeat(np.exp2(scales.astype(np.float64) - 127.0), 8, axis=1)[..., None]
    return vals.transpose(0, 1, 3, 2).reshape(g * 512, n)


K, T, S, G, H, W, C = 512, 1024, 256, 2048, 512, 128, 512


def setup_inputs():
    n = np.random.standard_normal
    s = mx_kscale(K)[:, None]
    packed_xT = pack_weight(n((K, T)) * s)
    packed_dT = pack_weight(n((K, G)) / s)
    perm = np.random.permutation(S)
    perm2 = np.random.permutation(S)
    perm3 = np.random.permutation(S)
    return {
        "x_words": packed_xT[0],
        "x_scales": packed_xT[1],
        "d_words": packed_dT[0],
        "d_scales": packed_dT[1],
        "gs": (np.random.uniform(0.5, 1.5, (K, 1)) / s).astype(np.float32),
        "offs": striped(np.random.permutation(T)[:S]),
        "k1": striped8(np.random.randint(0, G, (8, H))),
        "hz": striped8(np.random.randint(0, T, (8, S))),
        "k2": striped8(np.random.randint(0, G, (8, H))),
        "n1": striped(perm[:W]),
        "n2": striped(perm[W:]),
        "n3": striped(perm2[:W]),
        "n4": striped(perm2[W:]),
        "cand": striped8(np.random.randint(0, T, (8, C))),
        "n5": striped(perm3[:W]),
        "n6": striped(perm3[W:]),
        "n7": striped(np.random.permutation(S)),
    }


def reference(x_words, x_scales, d_words, d_scales, gs, offs, k1, hz, k2, n1, n2, n3, n4, cand, n5, n6, n7):
    x_cand = unpack_weight(x_words, x_scales)[np.arange(K)[:, None], runs(cand, K)]
    d_k1 = unpack_weight(d_words, d_scales)[np.arange(K)[:, None], runs(k1, K)]
    xq = unpack_weight(x_words, x_scales)[:, unstriped(offs)]
    d_k2 = unpack_weight(d_words, d_scales)[np.arange(K)[:, None], runs(k2, K)]
    x_hz = unpack_weight(x_words, x_scales)[np.arange(K)[:, None], runs(hz, K)]
    h = 0.0625 * (d_k1.T @ xq + d_k2.T @ x_hz)
    pa = h[:, unstriped(n1)]
    pb = h[:, unstriped(n2)]
    rb = pa - pb
    ra = np.maximum(pa, pb)
    ua = np.zeros((H, S))
    ua[:, unstriped(n3)] = ra
    ub = ua.copy()
    ub[:, unstriped(n4)] = rb
    z = f64(gs) * ub
    s = 0.0625 * ((x_cand.T @ mxq(z, 0, "e4m3")))
    pa2 = s[:, unstriped(n5)]
    pb2 = s[:, unstriped(n6)]
    rb2 = pa2 - pb2
    ua2 = np.zeros((C, S))
    ua2[:, unstriped(n5)] = pb2
    ub2 = ua2.copy()
    ub2[:, unstriped(n6)] = rb2
    return np.maximum(ub2, 0.5 * ub2[:, unstriped(n7)])

@@ -1,0 +1,205 @@
+from contextlib import ExitStack
+
+import concourse.mybir as mybir
+
+F32 = mybir.dt.float32
+BF16 = mybir.dt.bfloat16
+I32 = mybir.dt.int32
+U32 = mybir.dt.uint32
+U16 = mybir.dt.uint16
+U8 = mybir.dt.uint8
+FP8X4 = mybir.dt.float8_e4m3fn_x4
+ALU = mybir.AluOpType
+COPY = mybir.ActivationFunctionType.Copy
+
+P = 128
+PACK = 4
+K, T, S, G, H, W, C = 512, 1024, 256, 2048, 512, 128, 512
+SPARE = 16
+FLOPS = 2 * K * (2 * H * S + C * S)
+
+
+def tile_picked_mthzkcpmxswapd_none_p_kernel(
+    tc, x_words, x_scales, d_words, d_scales, gs, offs, k1, hz, k2, n1, n2, n3, n4, cand, n5, n6, n7, out
+):
+    nc = tc.nc
+    with ExitStack() as ctx:
+        keep = ctx.enter_context(tc.tile_pool(name="keep", bufs=1))
+        psum = ctx.enter_context(tc.psum_pool(name="psum", bufs=1))
+
+        def tile(name, shape, dtype):
+            return keep.tile(shape, dtype, name=name, align_bytes=64)
+
+        def load_list(name, ap):
+            t = keep.tile(list(ap.shape), U16, name=name)
+            nc.sync.dma_start(t[:], ap)
+            return t
+
+        d_bytes = tile("d_bytes", [P, G], U8)
+        x_bytes = tile("x_bytes", [P, T], U8)
+        nc.vector.memset(d_bytes[:].bitcast(I32), 0)
+        nc.vector.memset(x_bytes[:].bitcast(I32), 0)
+        nc.scalar.dma_start(d_bytes[0:P:8, :].bitcast(I32), d_scales[0].bitcast(I32))
+        nc.scalar.dma_start(x_bytes[0:P:8, :].bitcast(I32), x_scales[0].bitcast(I32))
+        k1_l = load_list("k1_l", k1)
+        k2_l = load_list("k2_l", k2)
+        hz_l = load_list("hz_l", hz)
+        offs_l = load_list("offs_l", offs)
+        x_tab = tile("x_tab", [P, T], U32)
+        d_tab = tile("d_tab", [P, G], U32)
+        nc.sync.dma_start(x_tab[:].bitcast(I32), x_words[0].rearrange("p n t -> p (n t)").bitcast(I32))
+        nc.sync.dma_start(d_tab[:].bitcast(I32), d_words[0].rearrange("p n t -> p (n t)").bitcast(I32))
+        n1_l = load_list("n1_l", n1)
+        n2_l = load_list("n2_l", n2)
+        n3_l = load_list("n3_l", n3)
+        n4_l = load_list("n4_l", n4)
+        cand_l = load_list("cand_l", cand)
+        gs_t = tile("gs_t", [P, PACK], F32)
+        nc.sync.dma_start(gs_t[:], gs.rearrange("(p t) o -> p (t o)", t=PACK))
+        n5_l = load_list("n5_l", n5)
+        n6_l = load_list("n6_l", n6)
+        n7_l = load_list("n7_l", n7)
+
+        def place_rows(plane, picked):
+            for q in range(4):
+                eng = nc.sync if q % 2 == 0 else nc.scalar
+                eng.dma_start(plane[32 * q : 32 * q + 4, :].bitcast(I32), picked[32 * q : 32 * q + 32 : 8, :].bitcast(I32))
+
+        hb = tile("hb", [P, 2 * H + 2 * S], U8)
+        h_plane = tile("h_plane", [P, 2 * H + 2 * S], U8)
+        c_plane = tile("c_plane", [P, C], U8)
+        nc.gpsimd.memset(h_plane[:].bitcast(I32), 0)
+        nc.gpsimd.memset(c_plane[:].bitcast(I32), 0)
+        nc.vector.tensor_copy(hb[:, 0:H], d_bytes[:].indirect(k1_l[:]))
+        nc.vector.tensor_copy(hb[:, H : 2 * H], d_bytes[:].indirect(k2_l[:]))
+        nc.vector.tensor_copy(hb[:, 2 * H : 2 * H + S], x_bytes[:].indirect(offs_l[:]))
+        nc.vector.tensor_copy(hb[:, 2 * H + S :], x_bytes[:].indirect(hz_l[:]))
+        place_rows(h_plane, hb)
+
+        xw = tile("xw", [P, 2 * S], U32)
+        dw = tile("dw", [P, 2 * H], U32)
+        nc.vector.tensor_copy(xw[:, 0:S], x_tab[:].indirect(offs_l[:]))
+        nc.vector.tensor_copy(xw[:, S:], x_tab[:].indirect(hz_l[:]))
+        nc.vector.tensor_copy(dw[:, 0:H], d_tab[:].indirect(k1_l[:]))
+        nc.vector.tensor_copy(dw[:, H:], d_tab[:].indirect(k2_l[:]))
+
+        cb = tile("cb", [P, C], U8)
+        cw = tile("cw", [P, C], U32)
+        z_bf = tile("z_bf", [P, S, PACK], BF16)
+
+        h_sb, pa, pb, ra, rb, ub = {}, {}, {}, {}, {}, {}
+
+        def product_h(t):
+            dealt_w = tile(f"dealt_w{t}", [P, 2 * P], U32)
+            dealt_b = tile(f"dealt_b{t}", [P, 2 * P], U8)
+            nc.vector.tensor_copy(dealt_w[:], dw[:, t : 2 * H : PACK])
+            nc.vector.tensor_copy(dealt_b[:], h_plane[:, t : 2 * H : PACK])
+            acc = psum.tile([P, S], F32, name=f"h_acc{t}")
+            for a in range(2):
+                nc.tensor.matmul_mx(
+                    out=acc[:],
+                    lhsT=dealt_w[:, a * P : (a + 1) * P].bitcast(FP8X4),
+                    lhsT_scale=dealt_b[:, a * P : (a + 1) * P],
+                    rhs=xw[:, a * S : (a + 1) * S].bitcast(FP8X4),
+                    rhs_scale=h_plane[:, 2 * H + a * S : 2 * H + (a + 1) * S],
+                    start=(a == 0),
+                    stop=(a == 1),
+                )
+            h_sb[t] = tile(f"h_sb{t}", [P, S], F32)
+            if t == 0:
+                nc.scalar.activation(h_sb[t][:], acc[:], COPY, scale=0.0625)
+            else:
+                nc.vector.tensor_scalar(h_sb[t][:], acc[:], 0.0625, None, ALU.mult)
+
+        def fetch_h(t):
+            pa[t] = tile(f"pa{t}", [P, W], F32)
+            pb[t] = tile(f"pb{t}", [P, W], F32)
+            nc.scalar.activation(pa[t][:], h_sb[t][:].indirect(n1_l[:]), COPY)
+            nc.scalar.activation(pb[t][:], h_sb[t][:].indirect(n2_l[:]), COPY)
+            ra[t] = tile(f"ra{t}", [P, W], F32)
+            rb[t] = tile(f"rb{t}", [P, W], F32)
+            nc.vector.tensor_tensor(ra[t][:], pa[t][:], pb[t][:], ALU.max)
+            nc.vector.tensor_tensor(rb[t][:], pa[t][:], pb[t][:], ALU.subtract)
+
+        def put_h(t):
+            ub[t] = tile(f"ub{t}", [P, S], F32)
+            nc.scalar.activation(ub[t][:].indirect(n3_l[:]), ra[t][:], COPY)
+            nc.scalar.activation(ub[t][:].indirect(n4_l[:]), rb[t][:], COPY)
+            nc.vector.tensor_scalar(z_bf[:, :, t], ub[t][:], gs_t[:, t : t + 1], None, ALU.mult)
+
+        def pick_cand(src, dst, half):
+            cols = slice(half * C // 2, (half + 1) * C // 2)
+            nc.vector.tensor_copy(dst[:, cols], src[:].indirect(cand_l[:, half * C // 32 : (half + 1) * C // 32]))
+
+        product_h(0)
+        fetch_h(0)
+        product_h(1)
+        fetch_h(1)
+        put_h(0)
+        product_h(2)
+        pick_cand(x_bytes, cb, 0)
+        pick_cand(x_bytes, cb, 1)
+        for q in range(4):
+            nc.sync.dma_start(c_plane[32 * q : 32 * q + 4, :].bitcast(I32), cb[32 * q : 32 * q + 32 : 8, :].bitcast(I32))
+        fetch_h(2)
+        put_h(1)
+        product_h(3)
+        pick_cand(x_tab, cw, 0)
+        fetch_h(3)
+        put_h(2)
+        pick_cand(x_tab, cw, 1)
+        put_h(3)
+
+        z_w = tile("z_w", [P, S], U32)
+        z_b = tile("z_b", [P, S], U8)
+        nc.vector.quantize_mx(out=z_w[:].bitcast(FP8X4), scales=z_b[:], in_=z_bf[:].rearrange("p j t -> p (j t)"))
+
+        s_sb, pa2, pb2, rb2, ub2 = {}, {}, {}, {}, {}
+        for b in range(4):
+            ub2[b] = tile(f"ub2_{b}", [P, S + SPARE], F32)
+            nc.gpsimd.memset(ub2[b][:, S:], 0.0)
+
+        def product_s(b):
+            acc = psum.tile([P, S], F32, name=f"s_acc{b}")
+            nc.tensor.matmul_mx(
+                out=acc[:],
+                lhsT=cw[:, b * P : (b + 1) * P].bitcast(FP8X4),
+                lhsT_scale=c_plane[:, b * P : (b + 1) * P],
+                rhs=z_w[:].bitcast(FP8X4),
+                rhs_scale=z_b[:],
+                start=True,
+                stop=True,
+            )
+            s_sb[b] = tile(f"s_sb{b}", [P, S], F32)
+            if b == 0:
+                nc.scalar.activation(s_sb[b][:], acc[:], COPY, scale=0.0625)
+            else:
+                nc.vector.tensor_scalar(s_sb[b][:], acc[:], 0.0625, None, ALU.mult)
+
+        def fetch_s(b):
+            pa2[b] = tile(f"pa2_{b}", [P, W], F32)
+            pb2[b] = tile(f"pb2_{b}", [P, W], F32)
+            rb2[b] = tile(f"rb2_{b}", [P, W], F32)
+            nc.scalar.activation(pb2[b][:], s_sb[b][:].indirect(n6_l[:]), COPY)
+            nc.scalar.activation(pa2[b][:], s_sb[b][:].indirect(n5_l[:]), COPY)
+            nc.vector.tensor_tensor(rb2[b][:], pa2[b][:], pb2[b][:], ALU.subtract)
+
+        def put_s(b):
+            nc.scalar.activation(ub2[b][:].indirect(n5_l[:]), pb2[b][:], COPY)
+            nc.scalar.activation(ub2[b][:].indirect(n6_l[:]), rb2[b][:], COPY)
+
+        def finish(b):
+            far = tile(f"far{b}", [P, S], F32)
+            res = tile(f"res{b}", [P, S], F32)
+            nc.scalar.activation(far[:], ub2[b][:].indirect(n7_l[:]), COPY)
+            nc.vector.scalar_tensor_tensor(res[:], far[:], 0.5, ub2[b][:, 0:S], ALU.mult, ALU.max)
+            nc.sync.dma_start(out[b * P : (b + 1) * P, :], res[:])
+
+        for b in range(4):
+            product_s(b)
+        for b in range(4):
+            fetch_s(b)
+            put_s(b)
+            if b > 0:
+                finish(b - 1)
+        finish(3)

@@ -27,8 +27,8 @@ def tile_picked_mthzkcpmxswapd_none_p_kernel(
         keep = ctx.enter_context(tc.tile_pool(name="keep", bufs=1))
         psum = ctx.enter_context(tc.psum_pool(name="psum", bufs=1))
 
-        def tile(name, shape, dtype):
-            return keep.tile(shape, dtype, name=name, align_bytes=64)
+        def tile(name, shape, dtype, tag=None, bufs=1):
+            return keep.tile(shape, dtype, name=name, tag=tag or name, bufs=bufs, align_bytes=64)
 
         def load_list(name, ap):
             t = keep.tile(list(ap.shape), U16, name=name)
@@ -37,17 +37,17 @@ def tile_picked_mthzkcpmxswapd_none_p_kernel(
 
         d_bytes = tile("d_bytes", [P, G], U8)
         x_bytes = tile("x_bytes", [P, T], U8)
+        nc.gpsimd.memset(x_bytes[:].bitcast(I32), 0)
+        nc.gpsimd.dma_start(x_bytes[0:P:8, :].bitcast(I32), x_scales[0].bitcast(I32))
         nc.vector.memset(d_bytes[:].bitcast(I32), 0)
-        nc.vector.memset(x_bytes[:].bitcast(I32), 0)
-        nc.scalar.dma_start(d_bytes[0:P:8, :].bitcast(I32), d_scales[0].bitcast(I32))
-        nc.scalar.dma_start(x_bytes[0:P:8, :].bitcast(I32), x_scales[0].bitcast(I32))
-        k1_l = load_list("k1_l", k1)
-        k2_l = load_list("k2_l", k2)
-        hz_l = load_list("hz_l", hz)
+        nc.gpsimd.dma_start(d_bytes[0:P:8, :].bitcast(I32), d_scales[0].bitcast(I32))
         offs_l = load_list("offs_l", offs)
+        hz_l = load_list("hz_l", hz)
         x_tab = tile("x_tab", [P, T], U32)
         d_tab = tile("d_tab", [P, G], U32)
         nc.sync.dma_start(x_tab[:].bitcast(I32), x_words[0].rearrange("p n t -> p (n t)").bitcast(I32))
+        k1_l = load_list("k1_l", k1)
+        k2_l = load_list("k2_l", k2)
         nc.sync.dma_start(d_tab[:].bitcast(I32), d_words[0].rearrange("p n t -> p (n t)").bitcast(I32))
         n1_l = load_list("n1_l", n1)
         n2_l = load_list("n2_l", n2)
@@ -55,50 +55,57 @@ def tile_picked_mthzkcpmxswapd_none_p_kernel(
         n4_l = load_list("n4_l", n4)
         cand_l = load_list("cand_l", cand)
         gs_t = tile("gs_t", [P, PACK], F32)
-        nc.sync.dma_start(gs_t[:], gs.rearrange("(p t) o -> p (t o)", t=PACK))
+        nc.gpsimd.dma_start(gs_t[:], gs.rearrange("(p t) o -> p (t o)", t=PACK))
         n5_l = load_list("n5_l", n5)
         n6_l = load_list("n6_l", n6)
         n7_l = load_list("n7_l", n7)
 
         def place_rows(plane, picked):
             for q in range(4):
-                eng = nc.sync if q % 2 == 0 else nc.scalar
+                eng = nc.sync
                 eng.dma_start(plane[32 * q : 32 * q + 4, :].bitcast(I32), picked[32 * q : 32 * q + 32 : 8, :].bitcast(I32))
 
         hb = tile("hb", [P, 2 * H + 2 * S], U8)
         h_plane = tile("h_plane", [P, 2 * H + 2 * S], U8)
         c_plane = tile("c_plane", [P, C], U8)
-        nc.gpsimd.memset(h_plane[:].bitcast(I32), 0)
-        nc.gpsimd.memset(c_plane[:].bitcast(I32), 0)
-        nc.vector.tensor_copy(hb[:, 0:H], d_bytes[:].indirect(k1_l[:]))
-        nc.vector.tensor_copy(hb[:, H : 2 * H], d_bytes[:].indirect(k2_l[:]))
-        nc.vector.tensor_copy(hb[:, 2 * H : 2 * H + S], x_bytes[:].indirect(offs_l[:]))
-        nc.vector.tensor_copy(hb[:, 2 * H + S :], x_bytes[:].indirect(hz_l[:]))
-        place_rows(h_plane, hb)
-
+        nc.vector.memset(h_plane[:].bitcast(I32), 0)
+        nc.vector.memset(c_plane[:].bitcast(I32), 0)
         xw = tile("xw", [P, 2 * S], U32)
-        dw = tile("dw", [P, 2 * H], U32)
         nc.vector.tensor_copy(xw[:, 0:S], x_tab[:].indirect(offs_l[:]))
         nc.vector.tensor_copy(xw[:, S:], x_tab[:].indirect(hz_l[:]))
+        nc.vector.tensor_copy(hb[:, 2 * H : 2 * H + S], x_bytes[:].indirect(offs_l[:]))
+        nc.vector.tensor_copy(hb[:, 2 * H + S :], x_bytes[:].indirect(hz_l[:]))
+        nc.vector.tensor_copy(hb[:, 0:H], d_bytes[:].indirect(k1_l[:]))
+        nc.vector.tensor_copy(hb[:, H : 2 * H], d_bytes[:].indirect(k2_l[:]))
+        place_rows(h_plane, hb)
+
+        dw = tile("dw", [P, 2 * H], U32, tag="d_bytes")
+        dealt_w = tile("dealt_w", [P, 2, PACK, P], U32)
+
+        def deal_words(a):
+            nc.vector.tensor_copy(
+                dealt_w[:, a].rearrange("p t m -> p m t"),
+                dw[:, a * H : (a + 1) * H].rearrange("p (m t) -> p m t", t=PACK),
+            )
+
         nc.vector.tensor_copy(dw[:, 0:H], d_tab[:].indirect(k1_l[:]))
         nc.vector.tensor_copy(dw[:, H:], d_tab[:].indirect(k2_l[:]))
+        deal_words(0)
 
-        cb = tile("cb", [P, C], U8)
-        cw = tile("cw", [P, C], U32)
         z_bf = tile("z_bf", [P, S, PACK], BF16)
 
         h_sb, pa, pb, ra, rb, ub = {}, {}, {}, {}, {}, {}
 
         def product_h(t):
-            dealt_w = tile(f"dealt_w{t}", [P, 2 * P], U32)
-            dealt_b = tile(f"dealt_b{t}", [P, 2 * P], U8)
-            nc.vector.tensor_copy(dealt_w[:], dw[:, t : 2 * H : PACK])
+            dealt_b = tile(f"dealt_b{t}", [P, 2 * P], U8, tag="dealt_b", bufs=2)
             nc.vector.tensor_copy(dealt_b[:], h_plane[:, t : 2 * H : PACK])
-            acc = psum.tile([P, S], F32, name=f"h_acc{t}")
+            acc = psum.tile([P, S], F32, name=f"h_acc{t}", tag=f"h_acc{t}")
             for a in range(2):
+                if t == 0 and a == 1:
+                    deal_words(1)
                 nc.tensor.matmul_mx(
                     out=acc[:],
-                    lhsT=dealt_w[:, a * P : (a + 1) * P].bitcast(FP8X4),
+                    lhsT=dealt_w[:, a, t, :].bitcast(FP8X4),
                     lhsT_scale=dealt_b[:, a * P : (a + 1) * P],
                     rhs=xw[:, a * S : (a + 1) * S].bitcast(FP8X4),
                     rhs_scale=h_plane[:, 2 * H + a * S : 2 * H + (a + 1) * S],
@@ -125,7 +132,10 @@ def tile_picked_mthzkcpmxswapd_none_p_kernel(
             ub[t] = tile(f"ub{t}", [P, S], F32)
             nc.scalar.activation(ub[t][:].indirect(n3_l[:]), ra[t][:], COPY)
             nc.scalar.activation(ub[t][:].indirect(n4_l[:]), rb[t][:], COPY)
-            nc.vector.tensor_scalar(z_bf[:, :, t], ub[t][:], gs_t[:, t : t + 1], None, ALU.mult)
+            parts = 2 if t == PACK - 1 else 1
+            for i in range(parts):
+                cols = slice(i * S // parts, (i + 1) * S // parts)
+                nc.vector.tensor_scalar(z_bf[:, cols, t], ub[t][:, cols], gs_t[:, t : t + 1], None, ALU.mult)
 
         def pick_cand(src, dst, half):
             cols = slice(half * C // 2, (half + 1) * C // 2)
@@ -137,6 +147,7 @@ def tile_picked_mthzkcpmxswapd_none_p_kernel(
         fetch_h(1)
         put_h(0)
         product_h(2)
+        cb = tile("cb", [P, C], U8, tag="h_sb0")
         pick_cand(x_bytes, cb, 0)
         pick_cand(x_bytes, cb, 1)
         for q in range(4):
@@ -144,6 +155,7 @@ def tile_picked_mthzkcpmxswapd_none_p_kernel(
         fetch_h(2)
         put_h(1)
         product_h(3)
+        cw = tile("cw", [P, C], U32, tag="h_sb1")
         pick_cand(x_tab, cw, 0)
         fetch_h(3)
         put_h(2)
@@ -152,54 +164,72 @@ def tile_picked_mthzkcpmxswapd_none_p_kernel(
 
         z_w = tile("z_w", [P, S], U32)
         z_b = tile("z_b", [P, S], U8)
-        nc.vector.quantize_mx(out=z_w[:].bitcast(FP8X4), scales=z_b[:], in_=z_bf[:].rearrange("p j t -> p (j t)"))
+        for i in range(2):
+            cols = slice(i * W, (i + 1) * W)
+            nc.vector.quantize_mx(
+                out=z_w[:, cols].bitcast(FP8X4), scales=z_b[:, cols], in_=z_bf[:, cols, :].rearrange("p j t -> p (j t)")
+            )
 
         s_sb, pa2, pb2, rb2, ub2 = {}, {}, {}, {}, {}
         for b in range(4):
             ub2[b] = tile(f"ub2_{b}", [P, S + SPARE], F32)
-            nc.gpsimd.memset(ub2[b][:, S:], 0.0)
+            nc.vector.memset(ub2[b][:, S:], 0.0)
 
         def product_s(b):
-            acc = psum.tile([P, S], F32, name=f"s_acc{b}")
-            nc.tensor.matmul_mx(
-                out=acc[:],
-                lhsT=cw[:, b * P : (b + 1) * P].bitcast(FP8X4),
-                lhsT_scale=c_plane[:, b * P : (b + 1) * P],
-                rhs=z_w[:].bitcast(FP8X4),
-                rhs_scale=z_b[:],
-                start=True,
-                stop=True,
-            )
             s_sb[b] = tile(f"s_sb{b}", [P, S], F32)
-            if b == 0:
-                nc.scalar.activation(s_sb[b][:], acc[:], COPY, scale=0.0625)
-            else:
-                nc.vector.tensor_scalar(s_sb[b][:], acc[:], 0.0625, None, ALU.mult)
+            parts = 2 if b == 0 else 1
+            for i in range(parts):
+                cols = slice(i * S // parts, (i + 1) * S // parts)
+                acc = psum.tile([P, S // parts], F32, name=f"s_acc{b}_{i}", tag=("h_acc0" if i else f"s_acc{b}"))
+                nc.tensor.matmul_mx(
+                    out=acc[:],
+                    lhsT=cw[:, b * P : (b + 1) * P].bitcast(FP8X4),
+                    lhsT_scale=c_plane[:, b * P : (b + 1) * P],
+                    rhs=z_w[:, cols].bitcast(FP8X4),
+                    rhs_scale=z_b[:, cols],
+                    start=True,
+                    stop=True,
+                )
+                if b == 0:
+                    nc.scalar.activation(s_sb[b][:, cols], acc[:], COPY, scale=0.0625)
+                else:
+                    nc.vector.tensor_scalar(s_sb[b][:, cols], acc[:], 0.0625, None, ALU.mult)
 
-        def fetch_s(b):
-            pa2[b] = tile(f"pa2_{b}", [P, W], F32)
-            pb2[b] = tile(f"pb2_{b}", [P, W], F32)
-            rb2[b] = tile(f"rb2_{b}", [P, W], F32)
+        def fetch_b(b):
+            pb2[b] = tile(f"pb2_{b}", [P, W], F32, tag="s_pb", bufs=2)
             nc.scalar.activation(pb2[b][:], s_sb[b][:].indirect(n6_l[:]), COPY)
+
+        def fetch_a(b):
+            pa2[b] = tile(f"pa2_{b}", [P, W], F32, tag="s_pa", bufs=2)
+            rb2[b] = tile(f"rb2_{b}", [P, W], F32, tag="s_rb", bufs=2)
             nc.scalar.activation(pa2[b][:], s_sb[b][:].indirect(n5_l[:]), COPY)
             nc.vector.tensor_tensor(rb2[b][:], pa2[b][:], pb2[b][:], ALU.subtract)
 
-        def put_s(b):
+        def put_b(b):
             nc.scalar.activation(ub2[b][:].indirect(n5_l[:]), pb2[b][:], COPY)
+
+        def put_r(b):
             nc.scalar.activation(ub2[b][:].indirect(n6_l[:]), rb2[b][:], COPY)
 
-        def finish(b):
+        def finish(b, parts):
             far = tile(f"far{b}", [P, S], F32)
             res = tile(f"res{b}", [P, S], F32)
-            nc.scalar.activation(far[:], ub2[b][:].indirect(n7_l[:]), COPY)
-            nc.vector.scalar_tensor_tensor(res[:], far[:], 0.5, ub2[b][:, 0:S], ALU.mult, ALU.max)
-            nc.sync.dma_start(out[b * P : (b + 1) * P, :], res[:])
+            w = S // parts
+            for i in range(parts):
+                cols = slice(i * w, (i + 1) * w)
+                nc.scalar.activation(far[:, cols], ub2[b][:].indirect(n7_l[:, i * w // 16 : (i + 1) * w // 16]), COPY)
+                nc.vector.scalar_tensor_tensor(res[:, cols], far[:, cols], 0.5, ub2[b][:, cols], ALU.mult, ALU.max)
+                nc.sync.dma_start(out[b * P : (b + 1) * P, cols], res[:, cols])
 
         for b in range(4):
             product_s(b)
+        fetch_b(0)
         for b in range(4):
-            fetch_s(b)
-            put_s(b)
+            fetch_a(b)
+            put_b(b)
             if b > 0:
-                finish(b - 1)
-        finish(3)
+                finish(b - 1, 1)
+            if b < 3:
+                fetch_b(b + 1)
+            put_r(b)
+        finish(3, 2)

@@ -37,17 +37,20 @@ def tile_picked_mthzkcpmxswapd_none_p_kernel(
 
         d_bytes = tile("d_bytes", [P, G], U8)
         x_bytes = tile("x_bytes", [P, T], U8)
-        nc.gpsimd.memset(x_bytes[:].bitcast(I32), 0)
-        nc.gpsimd.dma_start(x_bytes[0:P:8, :].bitcast(I32), x_scales[0].bitcast(I32))
-        nc.vector.memset(d_bytes[:].bitcast(I32), 0)
-        nc.gpsimd.dma_start(d_bytes[0:P:8, :].bitcast(I32), d_scales[0].bitcast(I32))
+
+        def load_scales(window, scales):
+            rows = scales[0].bitcast(I32)
+            nc.sync.dma_start(window[:].bitcast(I32), rows.unsqueeze(1).to_broadcast([16, 8, rows.shape[1]]))
+
+        load_scales(x_bytes, x_scales)
         offs_l = load_list("offs_l", offs)
         hz_l = load_list("hz_l", hz)
+        load_scales(d_bytes, d_scales)
+        k1_l = load_list("k1_l", k1)
+        k2_l = load_list("k2_l", k2)
         x_tab = tile("x_tab", [P, T], U32)
         d_tab = tile("d_tab", [P, G], U32)
         nc.sync.dma_start(x_tab[:].bitcast(I32), x_words[0].rearrange("p n t -> p (n t)").bitcast(I32))
-        k1_l = load_list("k1_l", k1)
-        k2_l = load_list("k2_l", k2)
         nc.sync.dma_start(d_tab[:].bitcast(I32), d_words[0].rearrange("p n t -> p (n t)").bitcast(I32))
         n1_l = load_list("n1_l", n1)
         n2_l = load_list("n2_l", n2)
@@ -70,42 +73,43 @@ def tile_picked_mthzkcpmxswapd_none_p_kernel(
         c_plane = tile("c_plane", [P, C], U8)
         nc.vector.memset(h_plane[:].bitcast(I32), 0)
         nc.vector.memset(c_plane[:].bitcast(I32), 0)
-        xw = tile("xw", [P, 2 * S], U32)
-        nc.vector.tensor_copy(xw[:, 0:S], x_tab[:].indirect(offs_l[:]))
-        nc.vector.tensor_copy(xw[:, S:], x_tab[:].indirect(hz_l[:]))
         nc.vector.tensor_copy(hb[:, 2 * H : 2 * H + S], x_bytes[:].indirect(offs_l[:]))
         nc.vector.tensor_copy(hb[:, 2 * H + S :], x_bytes[:].indirect(hz_l[:]))
         nc.vector.tensor_copy(hb[:, 0:H], d_bytes[:].indirect(k1_l[:]))
         nc.vector.tensor_copy(hb[:, H : 2 * H], d_bytes[:].indirect(k2_l[:]))
         place_rows(h_plane, hb)
 
-        dw = tile("dw", [P, 2 * H], U32, tag="d_bytes")
-        dealt_w = tile("dealt_w", [P, 2, PACK, P], U32)
+        hw = tile("hw", [P, 2 * H + 2 * S], U32, tag="d_bytes")
+        dw = hw[:, 0 : 2 * H]
+        xw = hw[:, 2 * H :]
+        nc.vector.tensor_copy(xw[:, 0:S], x_tab[:].indirect(offs_l[:]))
+        nc.vector.tensor_copy(xw[:, S:], x_tab[:].indirect(hz_l[:]))
+        dealt_w = {}
 
-        def deal_words(a):
+        def deal_words(t):
+            dealt_w[t] = tile(f"dealt_w{t}", [P, 2, 2, P], U32, tag="hb" if t else None)
             nc.vector.tensor_copy(
-                dealt_w[:, a].rearrange("p t m -> p m t"),
-                dw[:, a * H : (a + 1) * H].rearrange("p (m t) -> p m t", t=PACK),
+                dealt_w[t][:].rearrange("p a t m -> p a m t"),
+                dw.rearrange("p (a m t) -> p a m t", a=2, t=PACK)[:, :, :, t : t + 2],
             )
 
         nc.vector.tensor_copy(dw[:, 0:H], d_tab[:].indirect(k1_l[:]))
         nc.vector.tensor_copy(dw[:, H:], d_tab[:].indirect(k2_l[:]))
-        deal_words(0)
 
         z_bf = tile("z_bf", [P, S, PACK], BF16)
 
         h_sb, pa, pb, ra, rb, ub = {}, {}, {}, {}, {}, {}
 
         def product_h(t):
+            if t % 2 == 0:
+                deal_words(t)
             dealt_b = tile(f"dealt_b{t}", [P, 2 * P], U8, tag="dealt_b", bufs=2)
             nc.vector.tensor_copy(dealt_b[:], h_plane[:, t : 2 * H : PACK])
             acc = psum.tile([P, S], F32, name=f"h_acc{t}", tag=f"h_acc{t}")
             for a in range(2):
-                if t == 0 and a == 1:
-                    deal_words(1)
                 nc.tensor.matmul_mx(
                     out=acc[:],
-                    lhsT=dealt_w[:, a, t, :].bitcast(FP8X4),
+                    lhsT=dealt_w[t - t % 2][:, a, t % 2, :].bitcast(FP8X4),
                     lhsT_scale=dealt_b[:, a * P : (a + 1) * P],
                     rhs=xw[:, a * S : (a + 1) * S].bitcast(FP8X4),
                     rhs_scale=h_plane[:, 2 * H + a * S : 2 * H + (a + 1) * S],
@@ -223,13 +227,14 @@ def tile_picked_mthzkcpmxswapd_none_p_kernel(
 
         for b in range(4):
             product_s(b)
-        fetch_b(0)
         for b in range(4):
+            fetch_b(b)
             fetch_a(b)
             put_b(b)
             if b > 0:
-                finish(b - 1, 1)
-            if b < 3:
-                fetch_b(b + 1)
-            put_r(b)
+                put_r(b - 1)
+            if b > 1:
+                finish(b - 2, 1)
+        put_r(3)
+        finish(2, 1)
         finish(3, 2)

@@ -15,7 +15,12 @@ COPY = mybir.ActivationFunctionType.Copy
 P = 128
 PACK = 4
 K, T, S, G, H, W, C = 512, 1024, 256, 2048, 512, 128, 512
+BLOCKS = C // P
+SCALE_ROWS = K // 32
+GROUP = 16
+SIXTEENTH = 0.0625
 SPARE = 16
+LAST_SPLIT = 160
 FLOPS = 2 * K * (2 * H * S + C * S)
 
 
@@ -31,17 +36,30 @@ def tile_picked_mthzkcpmxswapd_none_p_kernel(
             return keep.tile(shape, dtype, name=name, tag=tag or name, bufs=bufs, align_bytes=64)
 
         def load_list(name, ap):
-            t = keep.tile(list(ap.shape), U16, name=name)
-            nc.sync.dma_start(t[:], ap)
-            return t
-
-        d_bytes = tile("d_bytes", [P, G], U8)
-        x_bytes = tile("x_bytes", [P, T], U8)
+            offsets = keep.tile(list(ap.shape), U16, name=name)
+            nc.sync.dma_start(offsets[:], ap)
+            return offsets
 
         def load_scales(window, scales):
             rows = scales[0].bitcast(I32)
-            nc.sync.dma_start(window[:].bitcast(I32), rows.unsqueeze(1).to_broadcast([16, 8, rows.shape[1]]))
+            nc.sync.dma_start(
+                window[:].bitcast(I32), rows.unsqueeze(1).to_broadcast([SCALE_ROWS, P // SCALE_ROWS, rows.shape[1]])
+            )
 
+        def place_rows(plane, picked):
+            for q in range(4):
+                nc.sync.dma_start(
+                    plane[32 * q : 32 * q + 4, :].bitcast(I32), picked[32 * q : 32 * q + 32 : 8, :].bitcast(I32)
+                )
+
+        def leave_psum(dst, acc, first):
+            if first:
+                nc.scalar.activation(dst, acc, COPY, scale=SIXTEENTH)
+            else:
+                nc.vector.tensor_scalar(dst, acc, SIXTEENTH, None, ALU.mult)
+
+        d_bytes = tile("d_bytes", [P, G], U8)
+        x_bytes = tile("x_bytes", [P, T], U8)
         load_scales(x_bytes, x_scales)
         offs_l = load_list("offs_l", offs)
         hz_l = load_list("hz_l", hz)
@@ -63,87 +81,86 @@ def tile_picked_mthzkcpmxswapd_none_p_kernel(
         n6_l = load_list("n6_l", n6)
         n7_l = load_list("n7_l", n7)
 
-        def place_rows(plane, picked):
-            for q in range(4):
-                eng = nc.sync
-                eng.dma_start(plane[32 * q : 32 * q + 4, :].bitcast(I32), picked[32 * q : 32 * q + 32 : 8, :].bitcast(I32))
-
-        hb = tile("hb", [P, 2 * H + 2 * S], U8)
+        h_bytes = tile("h_bytes", [P, 2 * H + 2 * S], U8)
         h_plane = tile("h_plane", [P, 2 * H + 2 * S], U8)
         c_plane = tile("c_plane", [P, C], U8)
         nc.vector.memset(h_plane[:].bitcast(I32), 0)
         nc.vector.memset(c_plane[:].bitcast(I32), 0)
-        nc.vector.tensor_copy(hb[:, 2 * H : 2 * H + S], x_bytes[:].indirect(offs_l[:]))
-        nc.vector.tensor_copy(hb[:, 2 * H + S :], x_bytes[:].indirect(hz_l[:]))
-        nc.vector.tensor_copy(hb[:, 0:H], d_bytes[:].indirect(k1_l[:]))
-        nc.vector.tensor_copy(hb[:, H : 2 * H], d_bytes[:].indirect(k2_l[:]))
-        place_rows(h_plane, hb)
+        nc.vector.tensor_copy(h_bytes[:, 2 * H : 2 * H + S], x_bytes[:].indirect(offs_l[:]))
+        nc.vector.tensor_copy(h_bytes[:, 2 * H + S :], x_bytes[:].indirect(hz_l[:]))
+        nc.vector.tensor_copy(h_bytes[:, 0:H], d_bytes[:].indirect(k1_l[:]))
+        nc.vector.tensor_copy(h_bytes[:, H : 2 * H], d_bytes[:].indirect(k2_l[:]))
+        place_rows(h_plane, h_bytes)
 
-        hw = tile("hw", [P, 2 * H + 2 * S], U32, tag="d_bytes")
-        dw = hw[:, 0 : 2 * H]
-        xw = hw[:, 2 * H :]
-        nc.vector.tensor_copy(xw[:, 0:S], x_tab[:].indirect(offs_l[:]))
-        nc.vector.tensor_copy(xw[:, S:], x_tab[:].indirect(hz_l[:]))
-        dealt_w = {}
-
-        def deal_words(t):
-            dealt_w[t] = tile(f"dealt_w{t}", [P, 2, 2, P], U32, tag="hb" if t else None)
-            nc.vector.tensor_copy(
-                dealt_w[t][:].rearrange("p a t m -> p a m t"),
-                dw.rearrange("p (a m t) -> p a m t", a=2, t=PACK)[:, :, :, t : t + 2],
-            )
-
-        nc.vector.tensor_copy(dw[:, 0:H], d_tab[:].indirect(k1_l[:]))
-        nc.vector.tensor_copy(dw[:, H:], d_tab[:].indirect(k2_l[:]))
+        h_words = tile("h_words", [P, 2 * H + 2 * S], U32, tag="d_bytes")
+        d_picked = h_words[:, 0 : 2 * H]
+        x_picked = h_words[:, 2 * H :]
+        nc.vector.tensor_copy(x_picked[:, 0:S], x_tab[:].indirect(offs_l[:]))
+        nc.vector.tensor_copy(x_picked[:, S:], x_tab[:].indirect(hz_l[:]))
+        nc.vector.tensor_copy(d_picked[:, 0:H], d_tab[:].indirect(k1_l[:]))
+        nc.vector.tensor_copy(d_picked[:, H:], d_tab[:].indirect(k2_l[:]))
 
         z_bf = tile("z_bf", [P, S, PACK], BF16)
+        dealt_words, h_sb, ra, rb = {}, {}, {}, {}
 
-        h_sb, pa, pb, ra, rb, ub = {}, {}, {}, {}, {}, {}
+        def deal_words(t, lists):
+            nc.vector.tensor_copy(
+                dealt_words[t][:, lists].rearrange("p a t m -> p a m t"),
+                d_picked.rearrange("p (a m t) -> p a m t", a=2, t=PACK)[:, lists, :, t : t + 2],
+            )
 
         def product_h(t):
+            first = t == 0
             if t % 2 == 0:
-                deal_words(t)
-            dealt_b = tile(f"dealt_b{t}", [P, 2 * P], U8, tag="dealt_b", bufs=2)
-            nc.vector.tensor_copy(dealt_b[:], h_plane[:, t : 2 * H : PACK])
-            acc = psum.tile([P, S], F32, name=f"h_acc{t}", tag=f"h_acc{t}")
-            for a in range(2):
-                nc.tensor.matmul_mx(
-                    out=acc[:],
-                    lhsT=dealt_w[t - t % 2][:, a, t % 2, :].bitcast(FP8X4),
-                    lhsT_scale=dealt_b[:, a * P : (a + 1) * P],
-                    rhs=xw[:, a * S : (a + 1) * S].bitcast(FP8X4),
-                    rhs_scale=h_plane[:, 2 * H + a * S : 2 * H + (a + 1) * S],
-                    start=(a == 0),
-                    stop=(a == 1),
-                )
+                dealt_words[t] = tile(f"dealt_words{t}", [P, 2, 2, P], U32, tag=None if first else "h_bytes")
+                deal_words(t, slice(0, 1 if first else 2))
+            dealt_bytes = tile(f"dealt_bytes{t}", [P, 2 * P], U8, tag="dealt_bytes", bufs=2)
+            nc.vector.tensor_copy(dealt_bytes[:], h_plane[:, t : 2 * H : PACK])
             h_sb[t] = tile(f"h_sb{t}", [P, S], F32)
-            if t == 0:
-                nc.scalar.activation(h_sb[t][:], acc[:], COPY, scale=0.0625)
-            else:
-                nc.vector.tensor_scalar(h_sb[t][:], acc[:], 0.0625, None, ALU.mult)
+            parts = 2 if first else 1
+            w = S // parts
+            accs = [
+                psum.tile([P, w], F32, name=f"h_acc{t}_{i}", tag=(f"s_acc{BLOCKS - 1}" if i else f"h_acc{t}"))
+                for i in range(parts)
+            ]
+            for a in range(2):
+                if first and a == 1:
+                    deal_words(0, slice(1, 2))
+                for i in range(parts):
+                    nc.tensor.matmul_mx(
+                        out=accs[i][:],
+                        lhsT=dealt_words[t - t % 2][:, a, t % 2, :].bitcast(FP8X4),
+                        lhsT_scale=dealt_bytes[:, a * P : (a + 1) * P],
+                        rhs=x_picked[:, a * S + i * w : a * S + (i + 1) * w].bitcast(FP8X4),
+                        rhs_scale=h_plane[:, 2 * H + a * S + i * w : 2 * H + a * S + (i + 1) * w],
+                        start=(a == 0),
+                        stop=(a == 1),
+                    )
+            for i in range(parts):
+                leave_psum(h_sb[t][:, i * w : (i + 1) * w], accs[i][:], first)
 
         def fetch_h(t):
-            pa[t] = tile(f"pa{t}", [P, W], F32)
-            pb[t] = tile(f"pb{t}", [P, W], F32)
-            nc.scalar.activation(pa[t][:], h_sb[t][:].indirect(n1_l[:]), COPY)
-            nc.scalar.activation(pb[t][:], h_sb[t][:].indirect(n2_l[:]), COPY)
+            pa = tile(f"pa{t}", [P, W], F32)
+            pb = tile(f"pb{t}", [P, W], F32)
+            nc.scalar.activation(pa[:], h_sb[t][:].indirect(n1_l[:]), COPY)
+            nc.scalar.activation(pb[:], h_sb[t][:].indirect(n2_l[:]), COPY)
             ra[t] = tile(f"ra{t}", [P, W], F32)
             rb[t] = tile(f"rb{t}", [P, W], F32)
-            nc.vector.tensor_tensor(ra[t][:], pa[t][:], pb[t][:], ALU.max)
-            nc.vector.tensor_tensor(rb[t][:], pa[t][:], pb[t][:], ALU.subtract)
+            nc.vector.tensor_tensor(ra[t][:], pa[:], pb[:], ALU.max)
+            nc.vector.tensor_tensor(rb[t][:], pa[:], pb[:], ALU.subtract)
 
         def put_h(t):
-            ub[t] = tile(f"ub{t}", [P, S], F32)
-            nc.scalar.activation(ub[t][:].indirect(n3_l[:]), ra[t][:], COPY)
-            nc.scalar.activation(ub[t][:].indirect(n4_l[:]), rb[t][:], COPY)
+            ub = tile(f"ub{t}", [P, S], F32)
+            nc.scalar.activation(ub[:].indirect(n3_l[:]), ra[t][:], COPY)
+            nc.scalar.activation(ub[:].indirect(n4_l[:]), rb[t][:], COPY)
             parts = 2 if t == PACK - 1 else 1
             for i in range(parts):
                 cols = slice(i * S // parts, (i + 1) * S // parts)
-                nc.vector.tensor_scalar(z_bf[:, cols, t], ub[t][:, cols], gs_t[:, t : t + 1], None, ALU.mult)
+                nc.vector.tensor_scalar(z_bf[:, cols, t], ub[:, cols], gs_t[:, t : t + 1], None, ALU.mult)
 
-        def pick_cand(src, dst, half):
-            cols = slice(half * C // 2, (half + 1) * C // 2)
-            nc.vector.tensor_copy(dst[:, cols], src[:].indirect(cand_l[:, half * C // 32 : (half + 1) * C // 32]))
+        def pick_cand(table, picked, half):
+            lo, hi = half * C // 2, (half + 1) * C // 2
+            nc.vector.tensor_copy(picked[:, lo:hi], table[:].indirect(cand_l[:, lo // GROUP : hi // GROUP]))
 
         product_h(0)
         fetch_h(0)
@@ -151,31 +168,32 @@ def tile_picked_mthzkcpmxswapd_none_p_kernel(
         fetch_h(1)
         put_h(0)
         product_h(2)
-        cb = tile("cb", [P, C], U8, tag="h_sb0")
-        pick_cand(x_bytes, cb, 0)
-        pick_cand(x_bytes, cb, 1)
-        for q in range(4):
-            nc.sync.dma_start(c_plane[32 * q : 32 * q + 4, :].bitcast(I32), cb[32 * q : 32 * q + 32 : 8, :].bitcast(I32))
+        c_bytes = tile("c_bytes", [P, C], U8, tag="h_sb1")
+        pick_cand(x_bytes, c_bytes, 0)
+        pick_cand(x_bytes, c_bytes, 1)
+        place_rows(c_plane, c_bytes)
         fetch_h(2)
         put_h(1)
         product_h(3)
-        cw = tile("cw", [P, C], U32, tag="h_sb1")
-        pick_cand(x_tab, cw, 0)
+        c_words = tile("c_words", [P, C], U32, tag="h_sb2")
+        pick_cand(x_tab, c_words, 0)
         fetch_h(3)
         put_h(2)
-        pick_cand(x_tab, cw, 1)
+        pick_cand(x_tab, c_words, 1)
         put_h(3)
 
-        z_w = tile("z_w", [P, S], U32)
-        z_b = tile("z_b", [P, S], U8)
+        z_words = tile("z_words", [P, S], U32)
+        z_plane = tile("z_plane", [P, S], U8)
         for i in range(2):
-            cols = slice(i * W, (i + 1) * W)
+            cols = slice(i * S // 2, (i + 1) * S // 2)
             nc.vector.quantize_mx(
-                out=z_w[:, cols].bitcast(FP8X4), scales=z_b[:, cols], in_=z_bf[:, cols, :].rearrange("p j t -> p (j t)")
+                out=z_words[:, cols].bitcast(FP8X4),
+                scales=z_plane[:, cols],
+                in_=z_bf[:, cols, :].rearrange("p j t -> p (j t)"),
             )
 
-        s_sb, pa2, pb2, rb2, ub2 = {}, {}, {}, {}, {}
-        for b in range(4):
+        s_sb, pb2, rb2, ub2 = {}, {}, {}, {}
+        for b in range(BLOCKS):
             ub2[b] = tile(f"ub2_{b}", [P, S + SPARE], F32)
             nc.vector.memset(ub2[b][:, S:], 0.0)
 
@@ -187,54 +205,46 @@ def tile_picked_mthzkcpmxswapd_none_p_kernel(
                 acc = psum.tile([P, S // parts], F32, name=f"s_acc{b}_{i}", tag=("h_acc0" if i else f"s_acc{b}"))
                 nc.tensor.matmul_mx(
                     out=acc[:],
-                    lhsT=cw[:, b * P : (b + 1) * P].bitcast(FP8X4),
+                    lhsT=c_words[:, b * P : (b + 1) * P].bitcast(FP8X4),
                     lhsT_scale=c_plane[:, b * P : (b + 1) * P],
-                    rhs=z_w[:, cols].bitcast(FP8X4),
-                    rhs_scale=z_b[:, cols],
+                    rhs=z_words[:, cols].bitcast(FP8X4),
+                    rhs_scale=z_plane[:, cols],
                     start=True,
                     stop=True,
                 )
-                if b == 0:
-                    nc.scalar.activation(s_sb[b][:, cols], acc[:], COPY, scale=0.0625)
-                else:
-                    nc.vector.tensor_scalar(s_sb[b][:, cols], acc[:], 0.0625, None, ALU.mult)
+                leave_psum(s_sb[b][:, cols], acc[:], b == 0)
 
-        def fetch_b(b):
+        def fetch_s(b):
             pb2[b] = tile(f"pb2_{b}", [P, W], F32, tag="s_pb", bufs=2)
             nc.scalar.activation(pb2[b][:], s_sb[b][:].indirect(n6_l[:]), COPY)
-
-        def fetch_a(b):
-            pa2[b] = tile(f"pa2_{b}", [P, W], F32, tag="s_pa", bufs=2)
+            pa2 = tile(f"pa2_{b}", [P, W], F32, tag="s_pa", bufs=2)
             rb2[b] = tile(f"rb2_{b}", [P, W], F32, tag="s_rb", bufs=2)
-            nc.scalar.activation(pa2[b][:], s_sb[b][:].indirect(n5_l[:]), COPY)
-            nc.vector.tensor_tensor(rb2[b][:], pa2[b][:], pb2[b][:], ALU.subtract)
+            nc.scalar.activation(pa2[:], s_sb[b][:].indirect(n5_l[:]), COPY)
+            nc.vector.tensor_tensor(rb2[b][:], pa2[:], pb2[b][:], ALU.subtract)
 
-        def put_b(b):
+        def put_pb2(b):
             nc.scalar.activation(ub2[b][:].indirect(n5_l[:]), pb2[b][:], COPY)
 
-        def put_r(b):
+        def put_rb2(b):
             nc.scalar.activation(ub2[b][:].indirect(n6_l[:]), rb2[b][:], COPY)
 
-        def finish(b, parts):
+        def finish(b, pieces):
             far = tile(f"far{b}", [P, S], F32)
             res = tile(f"res{b}", [P, S], F32)
-            w = S // parts
-            for i in range(parts):
-                cols = slice(i * w, (i + 1) * w)
-                nc.scalar.activation(far[:, cols], ub2[b][:].indirect(n7_l[:, i * w // 16 : (i + 1) * w // 16]), COPY)
-                nc.vector.scalar_tensor_tensor(res[:, cols], far[:, cols], 0.5, ub2[b][:, cols], ALU.mult, ALU.max)
-                nc.sync.dma_start(out[b * P : (b + 1) * P, cols], res[:, cols])
+            for lo, hi in pieces:
+                nc.scalar.activation(far[:, lo:hi], ub2[b][:].indirect(n7_l[:, lo // GROUP : hi // GROUP]), COPY)
+                nc.vector.scalar_tensor_tensor(res[:, lo:hi], far[:, lo:hi], 0.5, ub2[b][:, lo:hi], ALU.mult, ALU.max)
+                nc.sync.dma_start(out[b * P : (b + 1) * P, lo:hi], res[:, lo:hi])
 
-        for b in range(4):
+        for b in range(BLOCKS):
             product_s(b)
-        for b in range(4):
-            fetch_b(b)
-            fetch_a(b)
-            put_b(b)
+        for b in range(BLOCKS):
+            fetch_s(b)
+            put_pb2(b)
             if b > 0:
-                put_r(b - 1)
+                put_rb2(b - 1)
             if b > 1:
-                finish(b - 2, 1)
-        put_r(3)
-        finish(2, 1)
-        finish(3, 2)
+                finish(b - 2, [(0, S)])
+        put_rb2(BLOCKS - 1)
+        finish(BLOCKS - 2, [(0, S)])
+        finish(BLOCKS - 1, [(0, LAST_SPLIT), (LAST_SPLIT, S)])

from contextlib import ExitStack

import concourse.mybir as mybir

F32 = mybir.dt.float32
BF16 = mybir.dt.bfloat16
I32 = mybir.dt.int32
U32 = mybir.dt.uint32
U16 = mybir.dt.uint16
U8 = mybir.dt.uint8
FP8X4 = mybir.dt.float8_e4m3fn_x4
ALU = mybir.AluOpType
COPY = mybir.ActivationFunctionType.Copy

P = 128
PACK = 4
K, T, S, G, H, W, C = 512, 1024, 256, 2048, 512, 128, 512
BLOCKS = C // P
SCALE_ROWS = K // 32
GROUP = 16
SIXTEENTH = 0.0625
SPARE = 16
LAST_SPLIT = 160
FLOPS = 2 * K * (2 * H * S + C * S)


def tile_picked_mthzkcpmxswapd_none_p_kernel(
    tc, x_words, x_scales, d_words, d_scales, gs, offs, k1, hz, k2, n1, n2, n3, n4, cand, n5, n6, n7, out
):
    nc = tc.nc
    with ExitStack() as ctx:
        keep = ctx.enter_context(tc.tile_pool(name="keep", bufs=1))
        psum = ctx.enter_context(tc.psum_pool(name="psum", bufs=1))

        def tile(name, shape, dtype, tag=None, bufs=1):
            return keep.tile(shape, dtype, name=name, tag=tag or name, bufs=bufs, align_bytes=64)

        def load_list(name, ap):
            offsets = keep.tile(list(ap.shape), U16, name=name)
            nc.sync.dma_start(offsets[:], ap)
            return offsets

        def load_scales(window, scales):
            rows = scales[0].bitcast(I32)
            nc.sync.dma_start(
                window[:].bitcast(I32), rows.unsqueeze(1).to_broadcast([SCALE_ROWS, P // SCALE_ROWS, rows.shape[1]])
            )

        def place_rows(plane, picked):
            for q in range(4):
                nc.sync.dma_start(
                    plane[32 * q : 32 * q + 4, :].bitcast(I32), picked[32 * q : 32 * q + 32 : 8, :].bitcast(I32)
                )

        def leave_psum(dst, acc, first):
            if first:
                nc.scalar.activation(dst, acc, COPY, scale=SIXTEENTH)
            else:
                nc.vector.tensor_scalar(dst, acc, SIXTEENTH, None, ALU.mult)

        d_bytes = tile("d_bytes", [P, G], U8)
        x_bytes = tile("x_bytes", [P, T], U8)
        load_scales(x_bytes, x_scales)
        offs_l = load_list("offs_l", offs)
        hz_l = load_list("hz_l", hz)
        load_scales(d_bytes, d_scales)
        k1_l = load_list("k1_l", k1)
        k2_l = load_list("k2_l", k2)
        x_tab = tile("x_tab", [P, T], U32)
        d_tab = tile("d_tab", [P, G], U32)
        nc.sync.dma_start(x_tab[:].bitcast(I32), x_words[0].rearrange("p n t -> p (n t)").bitcast(I32))
        nc.sync.dma_start(d_tab[:].bitcast(I32), d_words[0].rearrange("p n t -> p (n t)").bitcast(I32))
        n1_l = load_list("n1_l", n1)
        n2_l = load_list("n2_l", n2)
        n3_l = load_list("n3_l", n3)
        n4_l = load_list("n4_l", n4)
        cand_l = load_list("cand_l", cand)
        gs_t = tile("gs_t", [P, PACK], F32)
        nc.gpsimd.dma_start(gs_t[:], gs.rearrange("(p t) o -> p (t o)", t=PACK))
        n5_l = load_list("n5_l", n5)
        n6_l = load_list("n6_l", n6)
        n7_l = load_list("n7_l", n7)

        h_bytes = tile("h_bytes", [P, 2 * H + 2 * S], U8)
        h_plane = tile("h_plane", [P, 2 * H + 2 * S], U8)
        c_plane = tile("c_plane", [P, C], U8)
        nc.vector.memset(h_plane[:].bitcast(I32), 0)
        nc.vector.memset(c_plane[:].bitcast(I32), 0)
        nc.vector.tensor_copy(h_bytes[:, 2 * H : 2 * H + S], x_bytes[:].indirect(offs_l[:]))
        nc.vector.tensor_copy(h_bytes[:, 2 * H + S :], x_bytes[:].indirect(hz_l[:]))
        nc.vector.tensor_copy(h_bytes[:, 0:H], d_bytes[:].indirect(k1_l[:]))
        nc.vector.tensor_copy(h_bytes[:, H : 2 * H], d_bytes[:].indirect(k2_l[:]))
        place_rows(h_plane, h_bytes)

        h_words = tile("h_words", [P, 2 * H + 2 * S], U32, tag="d_bytes")
        d_picked = h_words[:, 0 : 2 * H]
        x_picked = h_words[:, 2 * H :]
        nc.vector.tensor_copy(x_picked[:, 0:S], x_tab[:].indirect(offs_l[:]))
        nc.vector.tensor_copy(x_picked[:, S:], x_tab[:].indirect(hz_l[:]))
        nc.vector.tensor_copy(d_picked[:, 0:H], d_tab[:].indirect(k1_l[:]))
        nc.vector.tensor_copy(d_picked[:, H:], d_tab[:].indirect(k2_l[:]))

        z_bf = tile("z_bf", [P, S, PACK], BF16)
        dealt_words, h_sb, ra, rb = {}, {}, {}, {}

        def deal_words(t, lists):
            nc.vector.tensor_copy(
                dealt_words[t][:, lists].rearrange("p a t m -> p a m t"),
                d_picked.rearrange("p (a m t) -> p a m t", a=2, t=PACK)[:, lists, :, t : t + 2],
            )

        def product_h(t):
            first = t == 0
            if t % 2 == 0:
                dealt_words[t] = tile(f"dealt_words{t}", [P, 2, 2, P], U32, tag=None if first else "h_bytes")
                deal_words(t, slice(0, 1 if first else 2))
            dealt_bytes = tile(f"dealt_bytes{t}", [P, 2 * P], U8, tag="dealt_bytes", bufs=2)
            nc.vector.tensor_copy(dealt_bytes[:], h_plane[:, t : 2 * H : PACK])
            h_sb[t] = tile(f"h_sb{t}", [P, S], F32)
            parts = 2 if first else 1
            w = S // parts
            accs = [
                psum.tile([P, w], F32, name=f"h_acc{t}_{i}", tag=(f"s_acc{BLOCKS - 1}" if i else f"h_acc{t}"))
                for i in range(parts)
            ]
            for a in range(2):
                if first and a == 1:
                    deal_words(0, slice(1, 2))
                for i in range(parts):
                    nc.tensor.matmul_mx(
                        out=accs[i][:],
                        lhsT=dealt_words[t - t % 2][:, a, t % 2, :].bitcast(FP8X4),
                        lhsT_scale=dealt_bytes[:, a * P : (a + 1) * P],
                        rhs=x_picked[:, a * S + i * w : a * S + (i + 1) * w].bitcast(FP8X4),
                        rhs_scale=h_plane[:, 2 * H + a * S + i * w : 2 * H + a * S + (i + 1) * w],
                        start=(a == 0),
                        stop=(a == 1),
                    )
            for i in range(parts):
                leave_psum(h_sb[t][:, i * w : (i + 1) * w], accs[i][:], first)

        def fetch_h(t):
            pa = tile(f"pa{t}", [P, W], F32)
            pb = tile(f"pb{t}", [P, W], F32)
            nc.scalar.activation(pa[:], h_sb[t][:].indirect(n1_l[:]), COPY)
            nc.scalar.activation(pb[:], h_sb[t][:].indirect(n2_l[:]), COPY)
            ra[t] = tile(f"ra{t}", [P, W], F32)
            rb[t] = tile(f"rb{t}", [P, W], F32)
            nc.vector.tensor_tensor(ra[t][:], pa[:], pb[:], ALU.max)
            nc.vector.tensor_tensor(rb[t][:], pa[:], pb[:], ALU.subtract)

        def put_h(t):
            ub = tile(f"ub{t}", [P, S], F32)
            nc.scalar.activation(ub[:].indirect(n3_l[:]), ra[t][:], COPY)
            nc.scalar.activation(ub[:].indirect(n4_l[:]), rb[t][:], COPY)
            parts = 2 if t == PACK - 1 else 1
            for i in range(parts):
                cols = slice(i * S // parts, (i + 1) * S // parts)
                nc.vector.tensor_scalar(z_bf[:, cols, t], ub[:, cols], gs_t[:, t : t + 1], None, ALU.mult)

        def pick_cand(table, picked, half):
            lo, hi = half * C // 2, (half + 1) * C // 2
            nc.vector.tensor_copy(picked[:, lo:hi], table[:].indirect(cand_l[:, lo // GROUP : hi // GROUP]))

        product_h(0)
        fetch_h(0)
        product_h(1)
        fetch_h(1)
        put_h(0)
        product_h(2)
        c_bytes = tile("c_bytes", [P, C], U8, tag="h_sb1")
        pick_cand(x_bytes, c_bytes, 0)
        pick_cand(x_bytes, c_bytes, 1)
        place_rows(c_plane, c_bytes)
        fetch_h(2)
        put_h(1)
        product_h(3)
        c_words = tile("c_words", [P, C], U32, tag="h_sb2")
        pick_cand(x_tab, c_words, 0)
        fetch_h(3)
        put_h(2)
        pick_cand(x_tab, c_words, 1)
        put_h(3)

        z_words = tile("z_words", [P, S], U32)
        z_plane = tile("z_plane", [P, S], U8)
        for i in range(2):
            cols = slice(i * S // 2, (i + 1) * S // 2)
            nc.vector.quantize_mx(
                out=z_words[:, cols].bitcast(FP8X4),
                scales=z_plane[:, cols],
                in_=z_bf[:, cols, :].rearrange("p j t -> p (j t)"),
            )

        s_sb, pb2, rb2, ub2 = {}, {}, {}, {}
        for b in range(BLOCKS):
            ub2[b] = tile(f"ub2_{b}", [P, S + SPARE], F32)
            nc.vector.memset(ub2[b][:, S:], 0.0)

        def product_s(b):
            s_sb[b] = tile(f"s_sb{b}", [P, S], F32)
            parts = 2 if b == 0 else 1
            for i in range(parts):
                cols = slice(i * S // parts, (i + 1) * S // parts)
                acc = psum.tile([P, S // parts], F32, name=f"s_acc{b}_{i}", tag=("h_acc0" if i else f"s_acc{b}"))
                nc.tensor.matmul_mx(
                    out=acc[:],
                    lhsT=c_words[:, b * P : (b + 1) * P].bitcast(FP8X4),
                    lhsT_scale=c_plane[:, b * P : (b + 1) * P],
                    rhs=z_words[:, cols].bitcast(FP8X4),
                    rhs_scale=z_plane[:, cols],
                    start=True,
                    stop=True,
                )
                leave_psum(s_sb[b][:, cols], acc[:], b == 0)

        def fetch_s(b):
            pb2[b] = tile(f"pb2_{b}", [P, W], F32, tag="s_pb", bufs=2)
            nc.scalar.activation(pb2[b][:], s_sb[b][:].indirect(n6_l[:]), COPY)
            pa2 = tile(f"pa2_{b}", [P, W], F32, tag="s_pa", bufs=2)
            rb2[b] = tile(f"rb2_{b}", [P, W], F32, tag="s_rb", bufs=2)
            nc.scalar.activation(pa2[:], s_sb[b][:].indirect(n5_l[:]), COPY)
            nc.vector.tensor_tensor(rb2[b][:], pa2[:], pb2[b][:], ALU.subtract)

        def put_pb2(b):
            nc.scalar.activation(ub2[b][:].indirect(n5_l[:]), pb2[b][:], COPY)

        def put_rb2(b):
            nc.scalar.activation(ub2[b][:].indirect(n6_l[:]), rb2[b][:], COPY)

        def finish(b, pieces):
            far = tile(f"far{b}", [P, S], F32)
            res = tile(f"res{b}", [P, S], F32)
            for lo, hi in pieces:
                nc.scalar.activation(far[:, lo:hi], ub2[b][:].indirect(n7_l[:, lo // GROUP : hi // GROUP]), COPY)
                nc.vector.scalar_tensor_tensor(res[:, lo:hi], far[:, lo:hi], 0.5, ub2[b][:, lo:hi], ALU.mult, ALU.max)
                nc.sync.dma_start(out[b * P : (b + 1) * P, lo:hi], res[:, lo:hi])

        for b in range(BLOCKS):
            product_s(b)
        for b in range(BLOCKS):
            fetch_s(b)
            put_pb2(b)
            if b > 0:
                put_rb2(b - 1)
            if b > 1:
                finish(b - 2, [(0, S)])
        put_rb2(BLOCKS - 1)
        finish(BLOCKS - 2, [(0, S)])
        finish(BLOCKS - 1, [(0, LAST_SPLIT), (LAST_SPLIT, S)])
